import numpy as np
import ml_dtypes


def mxq(x, axis, fmt="e4m3"):
    dtype, down = {"e4m3": (ml_dtypes.float8_e4m3fn, 7), "e5m2": (ml_dtypes.float8_e5m2, 14)}[fmt]
    v = np.moveaxis(np.asarray(x, np.float32).astype(ml_dtypes.bfloat16).astype(np.float64), axis, -1)
    blocks = v.reshape(v.shape[:-1] + (-1, 32))
    amax = np.abs(blocks).max(-1, keepdims=True)
    byte = np.maximum(np.where(amax > 0, np.frexp(amax)[1] - 1 + 127, 0) - down, 1)
    scale = np.exp2(byte - 127.0)
    codes = (blocks / scale).astype(np.float32).astype(dtype).astype(np.float64)
    return np.moveaxis((codes * scale).reshape(v.shape), -1, axis)


WIDE = False


def mx_kscale(k):
    if not WIDE:
        return np.ones(k)
    levels = np.array([10, -10, 5, -5, 0])
    if k % 512:
        return np.exp2(np.random.permutation(np.resize(levels, k // 32))).repeat(32)
    a = np.empty((k // 512, 16))
    for p in range(k // 512):
        a[p, :8] = np.random.permutation(np.resize(levels, 8))
        for g in range(8):
            far = levels[np.abs(levels - a[p, g]) >= 10]
            a[p, g + 8] = far[np.random.randint(len(far))]
    return np.exp2(a.ravel()).repeat(32)


BF16 = ml_dtypes.bfloat16


def bf(x):
    return np.asarray(x, np.float32).astype(BF16)


def f64(x):
    return np.asarray(x).astype(np.float64)


B, J, K, M = 2048, 512, 1024, 512


def draw0():
    s, t = mx_kscale(J), mx_kscale(K)
    theta = np.random.standard_normal((B, J)) * s
    rho = np.random.standard_normal((B, J)) * 0.5 * s
    a = np.random.standard_normal((J, K)) / np.sqrt(J) / s[:, None]
    d1 = np.random.standard_normal(K) * 0.5
    g = (1.0 + 0.1 * np.random.standard_normal(K)) * t
    wr = np.random.standard_normal((K, M)) / np.sqrt(K) / t[:, None]
    wp = np.random.standard_normal((K, M)) / np.sqrt(K) / t[:, None]
    return {"theta": bf(theta), "rho": bf(rho), "a": bf(a), "d1": bf(d1), "g": bf(g), "wr": bf(wr), "wp": bf(wp)}


def interaction_phase(theta, aq, d1):
    return (mxq(f64(theta), 1, "e4m3") @ aq) + f64(d1)[None, :]


def interaction_modulus(rho, aq, g):
    q = mxq(f64(rho), 1, "e4m3") @ aq
    return np.exp(q) * f64(g)[None, :]


def core(theta, rho, a, d1, g, wr, wp):
    aq = mxq(f64(a), 0, "e4m3")
    psi = interaction_phase(theta, aq, d1)
    m = interaction_modulus(rho, aq, g)
    re = m * np.cos(psi)
    pe = m * np.sin(psi)
    y = (mxq(re, 1, "e4m3") @ mxq(f64(wr), 0, "e4m3")) + (mxq(pe, 1, "e4m3") @ mxq(f64(wp), 0, "e4m3"))
    return y


def e4m3fn_bytes(y):
    return np.clip(np.asarray(y, np.float64), -448.0, 448.0).astype(np.float32).astype(ml_dtypes.float8_e4m3fn).view(np.uint8)


def e4m3fn_values(b):
    return np.asarray(b, np.uint8).view(ml_dtypes.float8_e4m3fn).astype(np.float64)


def setup_inputs():
    d = draw0()
    x0 = np.asarray(d['theta']).astype(np.float64)
    s = (np.max(np.abs(x0), axis=(0,), keepdims=True) / 448.0).astype(np.float32)
    out = {}
    for k, v in d.items():
        if k == 'theta':
            out['theta_bytes'] = e4m3fn_bytes(x0 / s.astype(np.float64))
            out['theta_scale'] = s
        else:
            out[k] = v
    return out


def reference(theta_bytes, theta_scale, rho, a, d1, g, wr, wp):
    return core(e4m3fn_values(theta_bytes) * theta_scale.astype(np.float64), rho, a, d1, g, wr, wp)

import math
from contextlib import ExitStack

import concourse.mybir as mybir
from concourse.masks import make_identity

B, J, K, M = 2048, 512, 1024, 512
FLOPS = 2 * 2 * B * J * K + 2 * 2 * B * K * M

F32 = mybir.dt.float32
BF16 = mybir.dt.bfloat16
I32 = mybir.dt.int32
U32 = mybir.dt.uint32
U8 = mybir.dt.uint8
FP8 = mybir.dt.float8_e4m3fn
FP8X4 = mybir.dt.float8_e4m3fn_x4
ALU = mybir.AluOpType
ACT = mybir.ActivationFunctionType

P = 128
PACK = 4
CHUNK = 512
CHUNKS = B // CHUNK
TILES = CHUNK // P
GROUPS = K // (P * PACK)
BLOCKS = CHUNKS * GROUPS
TWO_PI = 2.0 * math.pi
KR = (0, 0, 2, 2, 2, 2, 2, 2, 2, 2, 1, 0, 0, 0, 0, 0, 0)
ON_GPSIMD = (2, 3, 4, 5, 6, 7, 8, 9)


def tile_eulerinteractionpolarlayer_kernel(tc, theta_bytes, theta_scale, rho, a, d1, g, wr, wp, out):
    nc = tc.nc
    rows_per_p = B // P
    th_in = theta_bytes.rearrange("(p i) k -> p i k", i=rows_per_p)
    rho_in = rho.rearrange("(p i) k -> p i k", i=rows_per_p)
    out_v = out.rearrange("(p i) n -> p i n", i=rows_per_p)
    a_in = a.rearrange("(p j) c -> p j c", j=PACK)
    w_in = [w.rearrange("(h p j) n -> h p j n", p=P, j=PACK) for w in (wr, wp)]

    with ExitStack() as ctx:
        keep = ctx.enter_context(tc.tile_pool(name="keep", bufs=1))
        sb = ctx.enter_context(tc.tile_pool(name="sb", bufs=2))
        ps = ctx.enter_context(tc.psum_pool(name="ps", bufs=2))
        ctx.enter_context(tc.manual_schedule(engines={mybir.EngineType.Activation}))

        th8 = {}

        def load_theta(c):
            t8 = sb.tile([P, TILES, J], U8, name="t8", tag="t8", bufs=3, align_bytes=64)
            nc.sync.dma_start(out=t8[:], in_=th_in[:, c * TILES : (c + 1) * TILES, :])
            th8[c] = t8

        rho_raw = {}

        def raw_tile():
            raw = sb.tile([P, 4, 512], BF16, name="raw", tag="raw", bufs=4, align_bytes=64)
            return raw

        def load_rho(c):
            rho_raw[c] = raw_tile()
            nc.sync.dma_start(out=rho_raw[c][:], in_=rho_in[:, c * TILES : (c + 1) * TILES, :])

        a_raw = []

        def load_a(h):
            ar = raw_tile()
            nc.sync.dma_start(out=ar[:], in_=a_in[:, :, h * 512 : (h + 1) * 512])
            a_raw.append(ar)

        load_a(0)
        scale_bc = keep.tile([P, J], F32, name="scale_bc", align_bytes=64)
        nc.sync.dma_start(out=scale_bc[:], in_=theta_scale.rearrange("o k -> (o k)").partition_broadcast(P))
        load_theta(0)
        load_rho(0)
        g_bf = keep.tile([P, GROUPS, PACK], BF16, name="g_bf")
        d_bf = keep.tile([P, GROUPS, PACK], BF16, name="d_bf")
        load_a(1)
        nc.sync.dma_start(out=g_bf[:], in_=g.rearrange("(h p t) -> p h t", p=P, t=PACK))
        nc.sync.dma_start(out=d_bf[:], in_=d1.rearrange("(h p t) -> p h t", p=P, t=PACK))
        load_rho(1)
        load_theta(1)

        ident = keep.tile([P, P], F32, name="ident")
        make_identity(nc, ident[:])

        NU = GROUPS * PACK
        gabs = keep.tile([P, NU], F32, name="gabs")
        gneg = keep.tile([P, NU], F32, name="gneg")
        lng = keep.tile([P, NU], F32, name="lng")
        dsin = keep.tile([P, NU], F32, name="dsin")
        warm = keep.tile([P, 2], F32, name="warm")
        nc.vector.memset(warm[:], 1.0)
        a_codes = keep.tile([P, GROUPS, 512], U32, name="a_codes", align_bytes=64)
        a_sc = keep.tile([P, GROUPS, 512], U8, name="a_sc", align_bytes=64)
        w_codes = keep.tile([P, 4, 512], U32, name="w_codes", align_bytes=64)
        w_sc = keep.tile([P, 4, 512], U8, name="w_sc", align_bytes=64)
        th_codes = keep.tile([P, CHUNKS, CHUNK], U32, name="th_codes", align_bytes=64)
        th_sc = keep.tile([P, CHUNKS, CHUNK], U8, name="th_sc", align_bytes=64)
        rho_codes = keep.tile([P, CHUNKS, CHUNK], U32, name="rho_codes", align_bytes=64)
        rho_sc = keep.tile([P, CHUNKS, CHUNK], U8, name="rho_sc", align_bytes=64)

        def grouped_tile():
            xg = sb.tile([P, 2048], BF16, name="xg", tag="xg", bufs=3, align_bytes=64)
            return xg

        def quantize(codes, scales, src):
            nc.vector.quantize_mx(out=codes.bitcast(FP8X4), scales=scales, in_=src)

        th16 = {}

        def widen_theta(c, half):
            if half == 0:
                th16[c] = sb.tile([P, TILES, J], BF16, name="th16", tag="th16", bufs=2, align_bytes=64)
            for i in range(2 * half, 2 * half + 2):
                nc.vector.tensor_tensor(out=th16[c][:, i, :], in0=th8[c][:, i, :].bitcast(FP8), in1=scale_bc[:], op=ALU.mult)

        turned = {}

        def turn(key, x, half):
            xt = ps.tile([P, 2, 256], F32, name="xt", tag="xt", bufs=2)
            for i in range(2):
                w = x[:, 2 * half + i, :].bitcast(F32)
                for u in range(2):
                    nc.tensor.transpose(xt[:, u, i * P : (i + 1) * P], w[:, u:256:2], ident[:])
            turned[key, half] = xt

        def group(key, half):
            if half == 0:
                turned[key] = grouped_tile()
            words = turned[key][:].bitcast(F32)
            nc.scalar.copy(out=words[:, half * 512 : (half + 1) * 512].rearrange("p (r u) -> p r u", u=2), in_=turned[key, half][:].rearrange("p u r -> p r u"))

        m_t = {}
        psi_t = {}
        k_t = {}
        r_t = {}
        c_t = {}

        q_t = {}

        def q_mm(b, t):
            c, h = divmod(b, GROUPS)
            acc = ps.tile([P, 512], F32, name="qo", tag="qo", bufs=3)
            nc.tensor.matmul_mx(out=acc[:], lhsT=a_codes[:, h, t * P : (t + 1) * P].bitcast(FP8X4), lhsT_scale=a_sc[:, h, t * P : (t + 1) * P],
                                rhs=rho_codes[:, c, :].bitcast(FP8X4), rhs_scale=rho_sc[:, c, :], start=True, stop=True)
            q_t[b, t] = acc

        def exp_unit(b, t):
            u = (b % GROUPS) * PACK + t
            if t == 0:
                m_t[b] = sb.tile([P, PACK, CHUNK], F32, name="m", tag="mr", bufs=12)
            nc.scalar.activation(out=m_t[b][:, t, :], in_=q_t[b, t][:], func=ACT.Exp, bias=lng[:, u : u + 1])

        def psi_mm(b, t):
            c, h = divmod(b, GROUPS)
            acc = ps.tile([P, 512], F32, name="psi", tag="psi", bufs=3)
            nc.tensor.matmul_mx(out=acc[:], lhsT=a_codes[:, h, t * P : (t + 1) * P].bitcast(FP8X4), lhsT_scale=a_sc[:, h, t * P : (t + 1) * P],
                                rhs=th_codes[:, c, :].bitcast(FP8X4), rhs_scale=th_sc[:, c, :], start=True, stop=True)
            psi_t[b, t] = acc

        def k_unit(b, t):
            u = (b % GROUPS) * PACK + t
            kk = sb.tile([P, 512], I32, name="kk", tag="kk", bufs=2)
            nc.vector.tensor_scalar(out=kk[:], in0=psi_t[b, t][:], scalar1=dsin[:, u : u + 1], scalar2=1.0 / TWO_PI, op0=ALU.add, op1=ALU.mult)
            k_t[b, t] = kk

        def r_unit(b, t):
            if t == 0:
                r_t[b] = sb.tile([P, PACK, CHUNK], F32, name="r", tag="mr", bufs=12)
            nc.vector.scalar_tensor_tensor(out=r_t[b][:, t, :], in0=k_t[b, t][:], scalar=-TWO_PI, in1=psi_t[b, t][:], op0=ALU.mult, op1=ALU.add)

        def abs_unit(b, t):
            u = (b % GROUPS) * PACK + t
            if t == 0:
                c_t[b] = sb.tile([P, PACK, CHUNK], F32, name="cs", tag="cs", bufs=3)
            nc.scalar.activation(out=c_t[b][:, t, :], in_=r_t[b][:, t, :], func=ACT.Abs, bias=dsin[:, u : u + 1])

        def cos_unit(b, lo, hi):
            nc.scalar.activation(out=c_t[b][:, lo:hi, :], in_=c_t[b][:, lo:hi, :], func=ACT.Sin, scale=-1.0, bias=math.pi / 2)

        def sin_unit(b, t):
            u = (b % GROUPS) * PACK + t
            nc.scalar.activation(out=r_t[b][:, t, :], in_=r_t[b][:, t, :], func=ACT.Sin, bias=dsin[:, u : u + 1])

        codes = {}

        def product_tile(lo, hi):
            pg = sb.tile([P, 2, (hi - lo) * PACK], BF16, name="pg", tag="pg", bufs=2, align_bytes=64)
            return pg

        def product(eng, pg, b, lo, hi, kind):
            trig = (c_t, r_t)[kind][b]
            tok = slice(lo, hi)
            eng.tensor_tensor(out=pg[:, kind, :].rearrange("p (c i t) -> p c t i", i=4, t=PACK),
                              in0=m_t[b][:, :, tok].rearrange("p t (c i) -> p c t i", i=4),
                              in1=trig[:, :, tok].rearrange("p t (c i) -> p c t i", i=4), op=ALU.mult)

        def quantize_product(pg, b, lo, hi):
            n = hi - lo
            cd = sb.tile([P, 2 * n], U32, name="pc", tag="pc", bufs=7, align_bytes=64)
            sc = sb.tile([P, 2 * n], U8, name="pk", tag="pk", bufs=7, align_bytes=64)
            quantize(cd[:], sc[:], pg[:].rearrange("p k w -> p (k w)"))
            for i in range(lo // P, hi // P):
                for kind in range(2):
                    codes[b, i, kind] = (cd, sc, kind * n + i * P - lo)

        outs = {}

        def out_mm(c, i):
            acc = ps.tile([P, 512], F32, name="qo2", tag="qo", bufs=3)
            n = 0
            for kind in range(2):
                for h in range(GROUPS):
                    cd, sc, at = codes[c * GROUPS + h, i, kind]
                    tok = slice(at, at + P)
                    w = kind * GROUPS + h
                    nc.tensor.matmul_mx(out=acc[:], lhsT=cd[:, tok].bitcast(FP8X4), lhsT_scale=sc[:, tok],
                                        rhs=w_codes[:, w, :].bitcast(FP8X4), rhs_scale=w_sc[:, w, :], start=(n == 0), stop=(n == 3))
                    n += 1
            outs[c, i] = acc

        def out_store(c, i, on_vector):
            o = sb.tile([P, M], F32, name="o", tag="o", bufs=3)
            if on_vector:
                nc.vector.tensor_copy(out=o[:], in_=outs[c, i][:])
            else:
                nc.scalar.copy(out=o[:], in_=outs[c, i][:])
            nc.sync.dma_start(out=out_v[:, c * TILES + i, :], in_=o[:])

        NK = BLOCKS * PACK

        def k_steps(lo, hi):
            for u in range(lo, hi):
                if u < NK:
                    k_unit(u // PACK, u % PACK)
                if u > 0:
                    r_unit((u - 1) // PACK, (u - 1) % PACK)
                if u + 2 < NK:
                    psi_mm((u + 2) // PACK, (u + 2) % PACK)

        def exps(lo, hi):
            for e in range(lo, hi):
                exp_unit(e // PACK, e % PACK)
                if e + 2 < Q_LIMIT[0]:
                    q_mm((e + 2) // PACK, (e + 2) % PACK)

        Q_LIMIT = [0]

        def q_ready(lo, hi):
            Q_LIMIT[0] = hi
            for e in range(lo, lo + 2):
                q_mm(e // PACK, e % PACK)

        def a_group(h):
            ag = grouped_tile()
            nc.vector.tensor_copy(out=ag[:].rearrange("p (t m j) -> p t m j", t=PACK, j=PACK), in_=a_raw[h][:].rearrange("p j (m t) -> p t m j", t=PACK))
            return ag

        def q_rho(c):
            quantize(rho_codes[:, c, :], rho_sc[:, c, :], turned["rho", c][:])

        def q_th(c):
            quantize(th_codes[:, c, :], th_sc[:, c, :], turned["th", c][:])

        def turns(kind, c):
            x = th16[c] if kind == "th" else rho_raw[c]
            turn((kind, c), x, 0)
            turn((kind, c), x, 1)

        def groups(kind, c):
            group((kind, c), 0)
            group((kind, c), 1)

        w_raw = []
        wg = []

        def load_weights():
            for j in range(4):
                wt = raw_tile()
                nc.sync.dma_start(out=wt[:], in_=w_in[j // 2][j % 2])
                w_raw.append(wt)

        def group_weights(j):
            xg = grouped_tile()
            nc.gpsimd.tensor_scalar(out=xg[:].rearrange("p (c i t) -> p c t i", i=4, t=PACK), in0=w_raw[j][:].rearrange("p t (c i) -> p c t i", i=4),
                                    scalar1=1.0, scalar2=0.0, op0=ALU.mult, op1=ALU.add)
            wg.append(xg)

        def quantize_weights(j):
            quantize(w_codes[:, j, :], w_sc[:, j, :], wg[j][:])

        def q_a(h, x):
            quantize(a_codes[:, h, :], a_sc[:, h, :], x[:])

        a0 = a_group(0)
        widen_theta(0, 0)
        turn(("th", 0), th16[0], 0)
        widen_theta(0, 1)
        turn(("th", 0), th16[0], 1)
        groups("th", 0)
        turns("rho", 0)
        groups("rho", 0)
        q_a(0, a0)
        q_th(0)
        a1 = a_group(1)
        psi_mm(0, 0)
        psi_mm(0, 1)
        g2 = g_bf[:].rearrange("p h t -> p (h t)")
        d2 = d_bf[:].rearrange("p h t -> p (h t)")
        nc.vector.tensor_scalar(out=gneg[:], in0=g2, scalar1=-1.0, scalar2=2.0 ** -64, op0=ALU.mult, op1=ALU.max)
        nc.vector.tensor_scalar(out=dsin[:], in0=g2, scalar1=0.0, scalar2=math.pi, op0=ALU.is_lt, op1=ALU.mult)
        nc.vector.tensor_tensor(out=gabs[:], in0=gneg[:], in1=g2, op=ALU.max)
        nc.vector.tensor_tensor(out=dsin[:], in0=dsin[:], in1=d2, op=ALU.add)

        nc.scalar.activation(out=lng[:], in_=gabs[:], func=ACT.Ln)
        nc.scalar.activation(out=warm[:, 0:1], in_=warm[:, 1:2], func=ACT.Exp)
        q_rho(0)
        q_ready(0, 8)
        k_steps(0, 1)
        exps(0, 2)
        q_a(1, a1)
        turns("rho", 1)
        k_steps(1, 2)
        exps(2, 4)
        groups("rho", 1)
        load_rho(2)
        load_theta(2)
        k_steps(2, 4)
        exps(4, 8)
        q_rho(1)
        q_ready(8, 16)
        widen_theta(1, 0)
        turns("rho", 2)
        exps(8, 9)
        groups("rho", 2)
        load_rho(3)
        load_theta(3)
        widen_theta(1, 1)
        k_steps(4, 5)
        turns("th", 1)
        exps(9, 11)
        groups("th", 1)
        q_rho(2)
        k_steps(5, 6)
        exps(11, 16)
        q_ready(16, 24)
        q_th(1)
        turns("rho", 3)
        exps(16, 17)
        groups("rho", 3)
        load_weights()
        k_steps(6, 8)
        exps(17, 20)
        widen_theta(2, 0)
        widen_theta(2, 1)
        turns("th", 2)
        exps(20, 22)
        groups("th", 2)
        q_rho(3)
        k_steps(8, 9)
        exps(22, 24)
        q_ready(24, 32)
        q_th(2)
        group_weights(0)
        k_steps(9, 11)
        exps(24, 28)
        widen_theta(3, 0)
        widen_theta(3, 1)
        turns("th", 3)
        exps(28, 30)
        groups("th", 3)
        exps(30, 32)
        k_steps(11, 12)
        for t in range(4):
            abs_unit(0, t)
        q_th(3)
        quantize_weights(0)
        group_weights(1)
        cos_unit(0, 0, 4)
        for t in range(PACK):
            sin_unit(0, t)
        k_steps(12, 14)
        quantize_weights(1)
        group_weights(2)
        group_weights(3)
        k_steps(14, 16)
        quantize_weights(2)
        quantize_weights(3)

        next_u = 16
        pend = None
        mm_wait = []
        ev_wait = []
        pieces = [(b, lo, lo + 256) for b in range(BLOCKS) for lo in (0, 256)]
        pieces[-1:] = [(BLOCKS - 1, 256, 384), (BLOCKS - 1, 384, 512)]
        for step in range(len(pieces)):
            b, lo, hi = pieces[step]
            part = lo // 256
            for j in range(KR[step]):
                k_steps(next_u, next_u + 1)
                next_u += 1
            if part == 0:
                for t in range(PACK):
                    if b == 0:
                        abs_unit(1, t)
                if b + 1 < BLOCKS:
                    cos_unit(b + 1, 0, 4)
            for t in range(part * 2, part * 2 + 2):
                if b + 2 < BLOCKS:
                    abs_unit(b + 2, t)
                if b + 1 < BLOCKS:
                    sin_unit(b + 1, t)
            pg = product_tile(lo, hi)
            product(nc.gpsimd if step in ON_GPSIMD else nc.vector, pg, b, lo, hi, 1)
            product(nc.vector, pg, b, lo, hi, 0)
            if pend is not None:
                quantize_product(*pend)
                if pend[1] % GROUPS == GROUPS - 1:
                    mm_wait += [(pend[1] // GROUPS, i) for i in range(pend[2] // P, pend[3] // P)]
            pend = (pg, b, lo, hi)
            while ev_wait:
                c, i = ev_wait.pop(0)
                out_store(c, i, False)
            while mm_wait:
                out_mm(*mm_wait[0])
                ev_wait.append(mm_wait.pop(0))
        quantize_product(*pend)
        for i in range(pend[2] // P, pend[3] // P):
            out_mm(pend[1] // GROUPS, i)
            ev_wait.append((pend[1] // GROUPS, i))
        for c, i in ev_wait:
            out_store(c, i, i % 2 == 0)
